import numpy as np
import ml_dtypes


def mxq(x, axis, fmt="e4m3"):
    dtype, down = {"e4m3": (ml_dtypes.float8_e4m3fn, 7), "e5m2": (ml_dtypes.float8_e5m2, 14)}[fmt]
    v = np.moveaxis(np.asarray(x, np.float32).astype(ml_dtypes.bfloat16).astype(np.float64), axis, -1)
    blocks = v.reshape(v.shape[:-1] + (-1, 32))
    amax = np.abs(blocks).max(-1, keepdims=True)
    byte = np.maximum(np.where(amax > 0, np.frexp(amax)[1] - 1 + 127, 0) - down, 1)
    scale = np.exp2(byte - 127.0)
    codes = (blocks / scale).astype(np.float32).astype(dtype).astype(np.float64)
    return np.moveaxis((codes * scale).reshape(v.shape), -1, axis)


WIDE = False


def mx_kscale(k):
    if not WIDE:
        return np.ones(k)
    levels = np.array([30, -30])
    if k % 512:
        return np.exp2(np.random.permutation(np.resize(levels, k // 32))).repeat(32)
    a = np.empty((k // 512, 16))
    for p in range(k // 512):
        a[p, :8] = np.random.permutation(np.resize(levels, 8))
        for g in range(8):
            far = levels[np.abs(levels - a[p, g]) >= 10]
            a[p, g + 8] = far[np.random.randint(len(far))]
    return np.exp2(a.ravel()).repeat(32)


def f64(x):
    return np.asarray(x).astype(np.float64)


def striped(idx):
    return np.tile(np.asarray(idx).reshape(-1, 16).T, (8, 1)).astype(np.uint16)


def unstriped(offs):
    return offs[:16].T.reshape(-1).astype(np.int64)


E2M1 = np.array([0.0, 0.5, 1.0, 1.5, 2.0, 3.0, 4.0, 6.0, -0.0, -0.5, -1.0, -1.5, -2.0, -3.0, -4.0, -6.0])


def pack_weight(w, fmt):
    k, n = w.shape
    w = f64(np.asarray(w, np.float32).astype(ml_dtypes.bfloat16)).reshape(k // 32, 32, n)
    amax = np.abs(w).max(1)
    if fmt in ("e4m3", "e5m2"):
        byte = np.frexp(amax)[1] - 1 + 127 - (7 if fmt == "e4m3" else 14)
    else:
        mant, ex = np.frexp(amax / 6.0)
        byte = np.where(mant > 0.5, ex, ex - 1) + 127
    byte = np.clip(np.where(amax > 0, byte, 1), 1, 254)
    scaled = (w * np.exp2(127.0 - byte)[:, None, :]).reshape(k, n).astype(np.float32)
    by_word = np.ascontiguousarray(scaled.reshape(k // 512, 128, 4, n).transpose(0, 1, 3, 2))
    if fmt in ("e4m3", "e5m2"):
        words = by_word.astype(ml_dtypes.float8_e4m3fn if fmt == "e4m3" else ml_dtypes.float8_e5m2).view(np.uint8)
    else:
        c = by_word.astype(ml_dtypes.float4_e2m1fn).view(np.uint8) & 0xF
        words = (c[..., 0::2] | (c[..., 1::2] << 4)).reshape(k // 512, 128, 2 * n)
    return np.ascontiguousarray(words), np.ascontiguousarray(byte.astype(np.uint8).reshape(k // 512, 16, n))


def unpack_weight(words, scales, fmt):
    g, _, n = scales.shape
    words = np.ascontiguousarray(words).reshape(g, 128, n, -1)
    if fmt in ("e4m3", "e5m2"):
        vals = words.view(ml_dtypes.float8_e4m3fn if fmt == "e4m3" else ml_dtypes.float8_e5m2).astype(np.float64)
    else:
        nib = np.empty((g, 128, n, 4), np.uint8)
        nib[..., 0::2] = words & 0xF
        nib[..., 1::2] = words >> 4
        vals = E2M1[nib]
    vals = vals * np.repeat(np.exp2(scales.astype(np.float64) - 127.0), 8, axis=1)[..., None]
    return vals.transpose(0, 1, 3, 2).reshape(g * 512, n)


K, T, J, R, F, Z, M, Q, C, O, N, S = 512, 1024, 256, 512, 512, 1024, 512, 128, 512, 128, 256, 1024


def setup_inputs():
    n = np.random.standard_normal
    idx = np.random.permutation(T)[:J]
    idx2 = np.random.permutation(Z)[:J]
    idx3 = np.random.permutation(C)[:Q]
    idx4 = np.random.permutation(C)[:O]
    idx5 = np.random.permutation(J)[:O]
    idx6 = np.random.permutation(J)[:O]
    idx7 = np.random.permutation(S)[:N]
    fk = mx_kscale(K)
    ff = mx_kscale(F)
    fm = mx_kscale(M)
    fr = mx_kscale(R)
    xtp = pack_weight(n((K, T)) / fk[:, None], "e2m1")
    xop = pack_weight(n((F, Z)) / ff[:, None], "e4m3")
    wp = pack_weight(n((K, R)) * 1 / np.sqrt(K) * fk[:, None], "e4m3")
    w0p = pack_weight(n((F, R)) * 1 / np.sqrt(F) * ff[:, None], "e2m1")
    xcp = pack_weight(n((M, Q)) / fm[:, None], "e4m3")
    wgp = pack_weight(n((M, R)) * 1 / np.sqrt(M) * fm[:, None] * fr, "e5m2")
    vsp = pack_weight(n((R, S)) * 1 / np.sqrt(R) / fr[:, None], "e2m1")
    return {
        "xt_words": xtp[0],
        "xt_scales": xtp[1],
        "xo_words": xop[0],
        "xo_scales": xop[1],
        "w_words": wp[0],
        "w_scales": wp[1],
        "w0_words": w0p[0],
        "w0_scales": w0p[1],
        "xc_words": xcp[0],
        "xc_scales": xcp[1],
        "wg_words": wgp[0],
        "wg_scales": wgp[1],
        "vs_words": vsp[0],
        "vs_scales": vsp[1],
        "offs": striped(idx),
        "offs2": striped(idx2),
        "offs3": striped(idx3),
        "offs4": striped(idx4),
        "offs5": striped(idx5),
        "offs6": striped(idx6),
        "offs7": striped(idx7),
    }


def reference(xt_words, xt_scales, xo_words, xo_scales, w_words, w_scales, w0_words, w0_scales, xc_words, xc_scales, wg_words, wg_scales, vs_words, vs_scales, offs, offs2, offs3, offs4, offs5, offs6, offs7):
    idx = unstriped(offs)
    idx2 = unstriped(offs2)
    idx3 = unstriped(offs3)
    idx4 = unstriped(offs4)
    idx5 = unstriped(offs5)
    idx6 = unstriped(offs6)
    idx7 = unstriped(offs7)
    xtu = unpack_weight(xt_words, xt_scales, "e2m1")
    xou = unpack_weight(xo_words, xo_scales, "e4m3")
    wu = unpack_weight(w_words, w_scales, "e4m3")
    w0u = unpack_weight(w0_words, w0_scales, "e2m1")
    xcu = unpack_weight(xc_words, xc_scales, "e4m3")
    wgu = unpack_weight(wg_words, wg_scales, "e5m2")
    vsu = unpack_weight(vs_words, vs_scales, "e2m1")
    xtidxg = xtu[:, idx]
    xoidx2g = xou[:, idx2]
    a = wu.T @ xtidxg + w0u.T @ xoidx2g
    g0 = wgu.T @ xcu
    ga = g0[:, 0:1]
    gb = g0[:, 64:65]
    pw = np.zeros((R, C))
    pw[:, idx3] = g0
    hid = np.maximum(a[:, idx5] * ga, a[:, idx6] * gb) - pw[:, idx4]
    vsidx7g = vsu[:, idx7]
    hidq = mxq(hid, 0, "e5m2")
    y = vsidx7g.T @ hidq
    return y

@@ -1,0 +1,194 @@
+from contextlib import ExitStack
+
+import concourse.mybir as mybir
+
+F32 = mybir.dt.float32
+BF16 = mybir.dt.bfloat16
+I32 = mybir.dt.int32
+U32 = mybir.dt.uint32
+U16 = mybir.dt.uint16
+U8 = mybir.dt.uint8
+E4M3 = mybir.dt.float8_e4m3fn_x4
+E5M2 = mybir.dt.float8_e5m2_x4
+E2M1 = mybir.dt.float4_e2m1fn_x4
+COPY = mybir.ActivationFunctionType.Copy
+ALU = mybir.AluOpType
+
+P = 128
+PACK = 4
+QUAD = 32
+T, J, R, Q, C, O, N = 1024, 256, 512, 128, 512, 128, 256
+FLOPS = 2 * 512 * (2 * R * J + R * Q + N * O)
+
+
+def tile_list_ctxboard_bank_store_plain_kernel(
+    tc, xt_words, xt_scales, xo_words, xo_scales, w_words, w_scales, w0_words, w0_scales,
+    xc_words, xc_scales, wg_words, wg_scales, vs_words, vs_scales,
+    offs, offs2, offs3, offs4, offs5, offs6, offs7, out,
+):
+    nc = tc.nc
+    with ExitStack() as ctx:
+        sb = ctx.enter_context(tc.tile_pool(name="sb", bufs=1))
+        ps = ctx.enter_context(tc.psum_pool(name="ps", bufs=1))
+
+        def tile(name, shape, dtype):
+            return sb.tile(shape, dtype, name=name, align_bytes=64)
+
+        def load_list(name, src):
+            lst = tile(name, list(src.shape), U16)
+            nc.sync.dma_start(lst[:], src)
+            return lst
+
+        def load_words8(name, src, queue=nc.sync):
+            words = tile(name, [P, src.shape[2]], U32)
+            queue.dma_start(words[:].bitcast(I32), src[0].rearrange("p n t -> p (n t)").bitcast(I32))
+            return words
+
+        def load_words4(name, src, queue=nc.sync):
+            words = tile(name, [P, src.shape[2] // 2], U16)
+            queue.dma_start(words[:].bitcast(I32), src[0].bitcast(I32))
+            return words
+
+        def zeroed(name, shape):
+            plane = tile(name, shape, U8)
+            nc.vector.memset(plane[:].bitcast(I32), 0)
+            return plane
+
+        def load_plane(plane, src):
+            rows = src[0].bitcast(I32)
+            for q in range(4):
+                nc.sync.dma_start(plane[QUAD * q : QUAD * q + 4, :].bitcast(I32), rows[4 * q : 4 * q + 4, :])
+
+        def staged(name, width):
+            stage = tile(name, [P, 4, width], U8)
+            nc.vector.memset(stage[:, 0, :].bitcast(I32), 0)
+            return stage
+
+        def load_stage(stage, col, src, queue=nc.sync):
+            rows = src[0].bitcast(I32).rearrange("(q r) n -> r q n", q=4)
+            queue.dma_start(stage[0:4, :, col : col + src.shape[2]].bitcast(I32), rows)
+
+        def spread(stage):
+            for q in range(1, 4):
+                nc.vector.tensor_copy(stage[QUAD * q : QUAD * q + 4, 0, :].bitcast(I32), stage[0:4, q, :].bitcast(I32))
+
+        def deal(copy, name, src, dtype):
+            dst = tile(name, [P, R], dtype)
+            copy(dst[:].rearrange("p (t m) -> p m t", t=PACK), src.rearrange("p (m t) -> p m t", t=PACK))
+            return dst
+
+        def gather(name, window, lst, width, dtype):
+            dst = tile(name, [P, width], dtype)
+            nc.vector.tensor_copy(dst[:], window[:].indirect(lst[:]))
+            return dst
+
+        g_both = staged("g_both", R + Q)
+        xt_plane = zeroed("xt_plane", [P, T])
+        a_both = staged("a_both", 2 * R)
+        xo_plane = zeroed("xo_plane", [P, T])
+        vs_plane = zeroed("vs_plane", [P, T])
+        board = [tile("board%d" % t, [P, C], F32) for t in range(PACK)]
+        for t in range(PACK):
+            nc.vector.memset(board[t][:], 0.0)
+
+        wg_raw = load_words8("wg_raw", wg_words, nc.scalar)
+        l1 = load_list("l1", offs)
+        xc = load_words8("xc", xc_words, nc.scalar)
+        load_stage(g_both, 0, wg_scales)
+        xt_tab = load_words4("xt_tab", xt_words, nc.scalar)
+        load_stage(g_both, R, xc_scales)
+        w_raw = load_words8("w_raw", w_words)
+        w0_raw = load_words4("w0_raw", w0_words)
+        load_stage(a_both, 0, w_scales)
+        load_stage(a_both, R, w0_scales)
+        load_plane(xt_plane, xt_scales)
+        xo_tab = load_words8("xo_tab", xo_words)
+        l2 = load_list("l2", offs2)
+        l3 = load_list("l3", offs3)
+        load_plane(xo_plane, xo_scales)
+        vs_tab = load_words4("vs_tab", vs_words)
+        l7 = load_list("l7", offs7)
+        load_plane(vs_plane, vs_scales)
+        l5 = load_list("l5", offs5)
+        l6 = load_list("l6", offs6)
+        l4 = load_list("l4", offs4)
+
+        spread(g_both)
+        wg = deal(nc.scalar.copy, "wg", wg_raw[:], U32)
+        wg_s = deal(nc.vector.tensor_copy, "wg_s", g_both[:, 0, 0:R], U8)
+        g_ps = ps.tile([P, PACK, Q], F32, name="g_ps")
+        for t in range(PACK):
+            cols = slice(t * P, (t + 1) * P)
+            nc.tensor.matmul_mx(
+                out=g_ps[:, t, :], lhsT=wg[:, cols].bitcast(E5M2), lhsT_scale=wg_s[:, cols],
+                rhs=xc[:].bitcast(E4M3), rhs_scale=g_both[:, 0, R : R + Q], start=True, stop=True,
+            )
+        g0 = tile("g0", [P, PACK, Q], F32)
+        nc.scalar.activation(g0[:], g_ps[:], COPY)
+
+        xt_g = gather("xt_g", xt_tab, l1, J, U16)
+        xt_gs = gather("xt_gs", xt_plane, l1, J, U8)
+        w = deal(nc.scalar.copy, "w", w_raw[:], U32)
+        spread(a_both)
+        w_s = deal(nc.vector.tensor_copy, "w_s", a_both[:, 0, 0:R], U8)
+        w0_s = deal(nc.vector.tensor_copy, "w0_s", a_both[:, 0, R : 2 * R], U8)
+        w0 = deal(nc.scalar.copy, "w0", w0_raw[:], U16)
+        xo_g = gather("xo_g", xo_tab, l2, J, U32)
+        xo_gs = gather("xo_gs", xo_plane, l2, J, U8)
+
+        vs_g = gather("vs_g", vs_tab, l7, N, U16)
+        vs_gs = gather("vs_gs", vs_plane, l7, N, U8)
+
+        for t in range(PACK):
+            nc.scalar.activation(board[t][:].indirect(l3[:]), g0[:, t, :], COPY)
+
+        a = []
+        for t in range(PACK):
+            cols = slice(t * P, (t + 1) * P)
+            a_ps = ps.tile([P, J], F32, name="a_ps%d" % t)
+            nc.tensor.matmul_mx(
+                out=a_ps[:], lhsT=w[:, cols].bitcast(E4M3), lhsT_scale=w_s[:, cols],
+                rhs=xt_g[:].bitcast(E2M1), rhs_scale=xt_gs[:], start=True, stop=False,
+            )
+            nc.tensor.matmul_mx(
+                out=a_ps[:], lhsT=w0[:, cols].bitcast(E2M1), lhsT_scale=w0_s[:, cols],
+                rhs=xo_g[:].bitcast(E4M3), rhs_scale=xo_gs[:], start=False, stop=True,
+            )
+            a_t = tile("a%d" % t, [P, J], F32)
+            nc.vector.tensor_copy(a_t[:], a_ps[:])
+            a.append(a_t)
+
+        picked = tile("picked", [P, PACK, O], F32)
+        first = tile("first", [P, PACK, O], F32)
+        second = tile("second", [P, PACK, O], F32)
+        larger = tile("larger", [P, PACK, O], F32)
+        hid = tile("hid", [P, O, PACK], BF16)
+        for t in range(PACK):
+            nc.vector.tensor_copy(picked[:, t, :], board[t][:].indirect(l4[:]))
+        for t in range(PACK):
+            nc.scalar.activation(first[:, t, :], a[t][:].indirect(l5[:]), COPY, scale=g0[:, t, 0:1])
+            nc.scalar.activation(second[:, t, :], a[t][:].indirect(l6[:]), COPY, scale=g0[:, t, 64:65])
+            nc.vector.tensor_tensor(larger[:, t, :], first[:, t, :], second[:, t, :], ALU.max)
+            if t % 2 == 1:
+                pair = slice(t - 1, t + 1)
+                nc.vector.tensor_tensor(
+                    hid[:, :, pair],
+                    larger[:, pair, :].rearrange("p t o -> p o t"),
+                    picked[:, pair, :].rearrange("p t o -> p o t"),
+                    ALU.subtract,
+                )
+
+        hid_q = tile("hid_q", [P, O], U32)
+        hid_s = tile("hid_s", [P, O], U8)
+        nc.vector.quantize_mx(out=hid_q[:].bitcast(E5M2), scales=hid_s[:], in_=hid[:].rearrange("p o t -> p (o t)"))
+
+        y = tile("y", [P, 2, O], F32)
+        for h, copy in enumerate((nc.scalar.copy, nc.vector.tensor_copy)):
+            cols = slice(h * P, (h + 1) * P)
+            y_ps = ps.tile([P, O], F32, name="y_ps%d" % h)
+            nc.tensor.matmul_mx(
+                out=y_ps[:], lhsT=vs_g[:, cols].bitcast(E2M1), lhsT_scale=vs_gs[:, cols],
+                rhs=hid_q[:].bitcast(E5M2), rhs_scale=hid_s[:], start=True, stop=True,
+            )
+            copy(y[:, h, :], y_ps[:])
+        nc.sync.dma_start(out.rearrange("(h p) o -> p h o", p=P), y[:])

@@ -16,9 +16,16 @@ ALU = mybir.AluOpType
 
 P = 128
 PACK = 4
-QUAD = 32
-T, J, R, Q, C, O, N = 1024, 256, 512, 128, 512, 128, 256
-FLOPS = 2 * 512 * (2 * R * J + R * Q + N * O)
+QUADS = 4
+QUAD = P // QUADS
+LIVE = 4
+PAIR = 2
+LINE_BYTES = 16
+CONTRACTION = P * PACK
+TABLE = 1024
+J, R, Q, C, O, N = 256, 512, 128, 512, 128, 256
+GB_COLUMN = 64
+FLOPS = 2 * CONTRACTION * (2 * R * J + R * Q + N * O)
 
 
 def tile_list_ctxboard_bank_store_plain_kernel(
@@ -28,167 +35,189 @@ def tile_list_ctxboard_bank_store_plain_kernel(
 ):
     nc = tc.nc
     with ExitStack() as ctx:
-        sb = ctx.enter_context(tc.tile_pool(name="sb", bufs=1))
-        ps = ctx.enter_context(tc.psum_pool(name="ps", bufs=1))
+        sbuf = ctx.enter_context(tc.tile_pool(name="sbuf", bufs=1))
+        psum = ctx.enter_context(tc.psum_pool(name="psum", bufs=1))
 
         def tile(name, shape, dtype):
-            return sb.tile(shape, dtype, name=name, align_bytes=64)
+            return sbuf.tile(shape, dtype, name=name, align_bytes=64)
+
+        def quadrant(q, rows):
+            return slice(QUAD * q, QUAD * q + rows)
+
+        def columns(i):
+            return slice(P * i, P * (i + 1))
+
+        def zeroed_plane(name, width):
+            plane = tile(name, [P, width], U8)
+            nc.vector.memset(plane[:].bitcast(I32), 0)
+            return plane
 
         def load_list(name, src):
-            lst = tile(name, list(src.shape), U16)
-            nc.sync.dma_start(lst[:], src)
-            return lst
+            offsets = tile(name, list(src.shape), U16)
+            nc.sync.dma_start(offsets[:], src)
+            return offsets
 
-        def load_words8(name, src, queue=nc.sync):
+        def load_fp8_words(name, src, queue):
             words = tile(name, [P, src.shape[2]], U32)
             queue.dma_start(words[:].bitcast(I32), src[0].rearrange("p n t -> p (n t)").bitcast(I32))
             return words
 
-        def load_words4(name, src, queue=nc.sync):
+        def load_fp4_words(name, src, queue):
             words = tile(name, [P, src.shape[2] // 2], U16)
             queue.dma_start(words[:].bitcast(I32), src[0].bitcast(I32))
             return words
 
-        def zeroed(name, shape):
-            plane = tile(name, shape, U8)
-            nc.vector.memset(plane[:].bitcast(I32), 0)
-            return plane
-
         def load_plane(plane, src):
-            rows = src[0].bitcast(I32)
-            for q in range(4):
-                nc.sync.dma_start(plane[QUAD * q : QUAD * q + 4, :].bitcast(I32), rows[4 * q : 4 * q + 4, :])
+            rows = src[0].bitcast(I32).rearrange("(q s) n -> s q n", s=LIVE)
+            for s in range(LIVE):
+                nc.sync.dma_start(plane[s:P:QUAD, :].bitcast(I32), rows[s])
 
-        def staged(name, width):
-            stage = tile(name, [P, 4, width], U8)
-            nc.vector.memset(stage[:, 0, :].bitcast(I32), 0)
-            return stage
+        def load_staged(stage, first_column, src):
+            rows = src[0].bitcast(I32).rearrange("(q s) n -> s q n", s=LIVE)
+            nc.sync.dma_start(stage[:, :, first_column : first_column + src.shape[2]].bitcast(I32), rows)
 
-        def load_stage(stage, col, src, queue=nc.sync):
-            rows = src[0].bitcast(I32).rearrange("(q r) n -> r q n", q=4)
-            queue.dma_start(stage[0:4, :, col : col + src.shape[2]].bitcast(I32), rows)
+        def move_rows(dst, src):
+            nc.vector.tensor_copy(dst.bitcast(I32), src.bitcast(I32))
 
-        def spread(stage):
-            for q in range(1, 4):
-                nc.vector.tensor_copy(stage[QUAD * q : QUAD * q + 4, 0, :].bitcast(I32), stage[0:4, q, :].bitcast(I32))
-
-        def deal(copy, name, src, dtype):
-            dst = tile(name, [P, R], dtype)
-            copy(dst[:].rearrange("p (t m) -> p m t", t=PACK), src.rearrange("p (m t) -> p m t", t=PACK))
-            return dst
-
-        def gather(name, window, lst, width, dtype):
-            dst = tile(name, [P, width], dtype)
-            nc.vector.tensor_copy(dst[:], window[:].indirect(lst[:]))
-            return dst
-
-        g_both = staged("g_both", R + Q)
-        xt_plane = zeroed("xt_plane", [P, T])
-        a_both = staged("a_both", 2 * R)
-        xo_plane = zeroed("xo_plane", [P, T])
-        vs_plane = zeroed("vs_plane", [P, T])
-        board = [tile("board%d" % t, [P, C], F32) for t in range(PACK)]
-        for t in range(PACK):
-            nc.vector.memset(board[t][:], 0.0)
-
-        wg_raw = load_words8("wg_raw", wg_words, nc.scalar)
-        l1 = load_list("l1", offs)
-        xc = load_words8("xc", xc_words, nc.scalar)
-        load_stage(g_both, 0, wg_scales)
-        xt_tab = load_words4("xt_tab", xt_words, nc.scalar)
-        load_stage(g_both, R, xc_scales)
-        w_raw = load_words8("w_raw", w_words)
-        w0_raw = load_words4("w0_raw", w0_words)
-        load_stage(a_both, 0, w_scales)
-        load_stage(a_both, R, w0_scales)
-        load_plane(xt_plane, xt_scales)
-        xo_tab = load_words8("xo_tab", xo_words)
-        l2 = load_list("l2", offs2)
-        l3 = load_list("l3", offs3)
-        load_plane(xo_plane, xo_scales)
-        vs_tab = load_words4("vs_tab", vs_words)
-        l7 = load_list("l7", offs7)
-        load_plane(vs_plane, vs_scales)
-        l5 = load_list("l5", offs5)
-        l6 = load_list("l6", offs6)
-        l4 = load_list("l4", offs4)
-
-        spread(g_both)
-        wg = deal(nc.scalar.copy, "wg", wg_raw[:], U32)
-        wg_s = deal(nc.vector.tensor_copy, "wg_s", g_both[:, 0, 0:R], U8)
-        g_ps = ps.tile([P, PACK, Q], F32, name="g_ps")
-        for t in range(PACK):
-            cols = slice(t * P, (t + 1) * P)
-            nc.tensor.matmul_mx(
-                out=g_ps[:, t, :], lhsT=wg[:, cols].bitcast(E5M2), lhsT_scale=wg_s[:, cols],
-                rhs=xc[:].bitcast(E4M3), rhs_scale=g_both[:, 0, R : R + Q], start=True, stop=True,
+        def deal_words(name, words, dtype, word_bytes):
+            dealt = tile(name, [P, R], dtype)
+            run = LINE_BYTES // word_bytes
+            nc.scalar.copy(
+                dealt[:].rearrange("p (t c i) -> p c t i", t=PACK, i=run),
+                words[:].rearrange("p (c i t) -> p c t i", t=PACK, i=run),
             )
+            return dealt
+
+        def deal_scales(name, engine, plane, first_slice, slices):
+            dealt = tile(name, [P, slices, P], U8)
+            by_slice = plane.rearrange("p (m t) -> p t m", t=PACK)
+            engine.tensor_copy(dealt[:], by_slice[:, first_slice : first_slice + slices, :])
+            return dealt
+
+        def gather(name, table, offsets, entries, dtype):
+            listed = tile(name, [P, entries], dtype)
+            nc.vector.tensor_copy(listed[:], table[:].indirect(offsets[:]))
+            return listed
+
+        home = 2
+        a_stage = tile("a_stage", [P, QUADS, 2 * R], U8)
+        nc.vector.memset(a_stage[QUAD * home : P, 0 : home + 1, :].bitcast(I32), 0)
+        g_plane = zeroed_plane("g_plane", R + Q)
+        g_stage = tile("g_stage", [LIVE, QUADS, R + Q], U8)
+        xt_plane = zeroed_plane("xt_plane", TABLE)
+        xo_plane = zeroed_plane("xo_plane", TABLE)
+        vs_plane = zeroed_plane("vs_plane", TABLE)
+        boards = [tile("board%d" % t, [P, C], F32) for t in range(PACK)]
+        for board in boards:
+            nc.vector.memset(board[:], 0.0)
+
+        load_staged(g_stage[:], 0, wg_scales)
+        wg_loaded = load_fp8_words("wg_loaded", wg_words, nc.scalar)
+        load_staged(g_stage[:], R, xc_scales)
+        w0_loaded = load_fp4_words("w0_loaded", w0_words, nc.scalar)
+        xc = load_fp8_words("xc", xc_words, nc.sync)
+        w_loaded = load_fp8_words("w_loaded", w_words, nc.scalar)
+        load_staged(a_stage[quadrant(home, LIVE)], 0, w_scales)
+        load_staged(a_stage[quadrant(home, LIVE)], R, w0_scales)
+        xt_table = load_fp4_words("xt_table", xt_words, nc.sync)
+        token_list = load_list("token_list", offs)
+        put_list = load_list("put_list", offs3)
+        load_plane(xt_plane, xt_scales)
+        xo_table = load_fp8_words("xo_table", xo_words, nc.sync)
+        note_list = load_list("note_list", offs2)
+        load_plane(xo_plane, xo_scales)
+        take_list = load_list("take_list", offs4)
+        vs_table = load_fp4_words("vs_table", vs_words, nc.sync)
+        store_list = load_list("store_list", offs7)
+        load_plane(vs_plane, vs_scales)
+        first_list = load_list("first_list", offs5)
+        second_list = load_list("second_list", offs6)
+
+        for q in range(QUADS):
+            move_rows(g_plane[quadrant(q, LIVE), :], g_stage[:, q, :])
+        wg = deal_words("wg", wg_loaded, U32, 4)
+        wg_scale = [
+            deal_scales("wg_scale%d" % h, engine, g_plane[:, 0:R], PAIR * h, PAIR)
+            for h, engine in enumerate((nc.vector, nc.gpsimd))
+        ]
         g0 = tile("g0", [P, PACK, Q], F32)
-        nc.scalar.activation(g0[:], g_ps[:], COPY)
+        for h in range(PACK // PAIR):
+            g_sums = psum.tile([P, PAIR, Q], F32, name="g_sums%d" % h)
+            for u in range(PAIR):
+                nc.tensor.matmul_mx(
+                    out=g_sums[:, u, :],
+                    lhsT=wg[:, columns(PAIR * h + u)].bitcast(E5M2), lhsT_scale=wg_scale[h][:, u, :],
+                    rhs=xc[:].bitcast(E4M3), rhs_scale=g_plane[:, R : R + Q], start=True, stop=True,
+                )
+            nc.scalar.activation(g0[:, PAIR * h : PAIR * (h + 1), :], g_sums[:], COPY)
 
-        xt_g = gather("xt_g", xt_tab, l1, J, U16)
-        xt_gs = gather("xt_gs", xt_plane, l1, J, U8)
-        w = deal(nc.scalar.copy, "w", w_raw[:], U32)
-        spread(a_both)
-        w_s = deal(nc.vector.tensor_copy, "w_s", a_both[:, 0, 0:R], U8)
-        w0_s = deal(nc.vector.tensor_copy, "w0_s", a_both[:, 0, R : 2 * R], U8)
-        w0 = deal(nc.scalar.copy, "w0", w0_raw[:], U16)
-        xo_g = gather("xo_g", xo_tab, l2, J, U32)
-        xo_gs = gather("xo_gs", xo_plane, l2, J, U8)
+        xt_listed = gather("xt_listed", xt_table, token_list, J, U16)
+        xt_scale = gather("xt_scale", xt_plane, token_list, J, U8)
+        w = deal_words("w", w_loaded, U32, 4)
+        for q in range(home):
+            move_rows(a_stage[quadrant(q, QUAD), home, :], a_stage[quadrant(home, QUAD), q, :])
+        move_rows(a_stage[quadrant(home + 1, LIVE), home, :], a_stage[quadrant(home, LIVE), home + 1, :])
+        w_scale = deal_scales("w_scale", nc.gpsimd, a_stage[:, home, 0:R], 0, PACK)
+        w0_scale = deal_scales("w0_scale", nc.gpsimd, a_stage[:, home, R : 2 * R], 0, PACK)
+        w0 = deal_words("w0", w0_loaded, U16, 2)
+        xo_listed = gather("xo_listed", xo_table, note_list, J, U32)
+        xo_scale = gather("xo_scale", xo_plane, note_list, J, U8)
 
-        vs_g = gather("vs_g", vs_tab, l7, N, U16)
-        vs_gs = gather("vs_gs", vs_plane, l7, N, U8)
+        vs_listed = gather("vs_listed", vs_table, store_list, N, U16)
+        vs_scale = gather("vs_scale", vs_plane, store_list, N, U8)
 
         for t in range(PACK):
-            nc.scalar.activation(board[t][:].indirect(l3[:]), g0[:, t, :], COPY)
+            nc.scalar.activation(boards[t][:].indirect(put_list[:]), g0[:, t, :], COPY)
 
         a = []
         for t in range(PACK):
-            cols = slice(t * P, (t + 1) * P)
-            a_ps = ps.tile([P, J], F32, name="a_ps%d" % t)
+            a_sums = psum.tile([P, J], F32, name="a_sums%d" % t)
             nc.tensor.matmul_mx(
-                out=a_ps[:], lhsT=w[:, cols].bitcast(E4M3), lhsT_scale=w_s[:, cols],
-                rhs=xt_g[:].bitcast(E2M1), rhs_scale=xt_gs[:], start=True, stop=False,
+                out=a_sums[:], lhsT=w[:, columns(t)].bitcast(E4M3), lhsT_scale=w_scale[:, t, :],
+                rhs=xt_listed[:].bitcast(E2M1), rhs_scale=xt_scale[:], start=True, stop=False,
             )
             nc.tensor.matmul_mx(
-                out=a_ps[:], lhsT=w0[:, cols].bitcast(E2M1), lhsT_scale=w0_s[:, cols],
-                rhs=xo_g[:].bitcast(E4M3), rhs_scale=xo_gs[:], start=False, stop=True,
+                out=a_sums[:], lhsT=w0[:, columns(t)].bitcast(E2M1), lhsT_scale=w0_scale[:, t, :],
+                rhs=xo_listed[:].bitcast(E4M3), rhs_scale=xo_scale[:], start=False, stop=True,
             )
-            a_t = tile("a%d" % t, [P, J], F32)
-            nc.vector.tensor_copy(a_t[:], a_ps[:])
-            a.append(a_t)
+            a_slice = tile("a%d" % t, [P, J], F32)
+            nc.vector.tensor_copy(a_slice[:], a_sums[:])
+            a.append(a_slice)
 
-        picked = tile("picked", [P, PACK, O], F32)
+        taken = tile("taken", [P, PACK, O], F32)
         first = tile("first", [P, PACK, O], F32)
         second = tile("second", [P, PACK, O], F32)
         larger = tile("larger", [P, PACK, O], F32)
         hid = tile("hid", [P, O, PACK], BF16)
         for t in range(PACK):
-            nc.vector.tensor_copy(picked[:, t, :], board[t][:].indirect(l4[:]))
-        for t in range(PACK):
-            nc.scalar.activation(first[:, t, :], a[t][:].indirect(l5[:]), COPY, scale=g0[:, t, 0:1])
-            nc.scalar.activation(second[:, t, :], a[t][:].indirect(l6[:]), COPY, scale=g0[:, t, 64:65])
-            nc.vector.tensor_tensor(larger[:, t, :], first[:, t, :], second[:, t, :], ALU.max)
-            if t % 2 == 1:
-                pair = slice(t - 1, t + 1)
-                nc.vector.tensor_tensor(
-                    hid[:, :, pair],
-                    larger[:, pair, :].rearrange("p t o -> p o t"),
-                    picked[:, pair, :].rearrange("p t o -> p o t"),
-                    ALU.subtract,
+            nc.vector.tensor_copy(taken[:, t, :], boards[t][:].indirect(take_list[:]))
+        for h in range(PACK // PAIR):
+            pair = slice(PAIR * h, PAIR * (h + 1))
+            for t in range(pair.start, pair.stop):
+                nc.scalar.activation(first[:, t, :], a[t][:].indirect(first_list[:]), COPY, scale=g0[:, t, 0:1])
+                nc.scalar.activation(
+                    second[:, t, :], a[t][:].indirect(second_list[:]), COPY, scale=g0[:, t, GB_COLUMN : GB_COLUMN + 1]
                 )
-
-        hid_q = tile("hid_q", [P, O], U32)
-        hid_s = tile("hid_s", [P, O], U8)
-        nc.vector.quantize_mx(out=hid_q[:].bitcast(E5M2), scales=hid_s[:], in_=hid[:].rearrange("p o t -> p (o t)"))
-
-        y = tile("y", [P, 2, O], F32)
-        for h, copy in enumerate((nc.scalar.copy, nc.vector.tensor_copy)):
-            cols = slice(h * P, (h + 1) * P)
-            y_ps = ps.tile([P, O], F32, name="y_ps%d" % h)
-            nc.tensor.matmul_mx(
-                out=y_ps[:], lhsT=vs_g[:, cols].bitcast(E2M1), lhsT_scale=vs_gs[:, cols],
-                rhs=hid_q[:].bitcast(E5M2), rhs_scale=hid_s[:], start=True, stop=True,
+                nc.vector.tensor_tensor(larger[:, t, :], first[:, t, :], second[:, t, :], ALU.max)
+            nc.vector.tensor_tensor(
+                hid[:, :, pair],
+                larger[:, pair, :].rearrange("p t o -> p o t"),
+                taken[:, pair, :].rearrange("p t o -> p o t"),
+                ALU.subtract,
             )
-            copy(y[:, h, :], y_ps[:])
-        nc.sync.dma_start(out.rearrange("(h p) o -> p h o", p=P), y[:])
+
+        hid_words = tile("hid_words", [P, O], U32)
+        hid_scale = tile("hid_scale", [P, O], U8)
+        nc.vector.quantize_mx(
+            out=hid_words[:].bitcast(E5M2), scales=hid_scale[:], in_=hid[:].rearrange("p o t -> p (o t)")
+        )
+
+        y = tile("y", [P, N // P, O], F32)
+        for half, (copy, queue) in enumerate(((nc.vector.tensor_copy, nc.sync), (nc.scalar.copy, nc.scalar))):
+            y_sums = psum.tile([P, O], F32, name="y_sums%d" % half)
+            nc.tensor.matmul_mx(
+                out=y_sums[:], lhsT=vs_listed[:, columns(half)].bitcast(E2M1), lhsT_scale=vs_scale[:, columns(half)],
+                rhs=hid_words[:].bitcast(E5M2), rhs_scale=hid_scale[:], start=True, stop=True,
+            )
+            copy(y[:, half, :], y_sums[:])
+            queue.dma_start(out[columns(half), :], y[:, half, :])

from contextlib import ExitStack

import concourse.mybir as mybir

F32 = mybir.dt.float32
BF16 = mybir.dt.bfloat16
I32 = mybir.dt.int32
U32 = mybir.dt.uint32
U16 = mybir.dt.uint16
U8 = mybir.dt.uint8
E4M3 = mybir.dt.float8_e4m3fn_x4
E5M2 = mybir.dt.float8_e5m2_x4
E2M1 = mybir.dt.float4_e2m1fn_x4
COPY = mybir.ActivationFunctionType.Copy
ALU = mybir.AluOpType

P = 128
PACK = 4
QUADS = 4
QUAD = P // QUADS
LIVE = 4
PAIR = 2
LINE_BYTES = 16
CONTRACTION = P * PACK
TABLE = 1024
J, R, Q, C, O, N = 256, 512, 128, 512, 128, 256
GB_COLUMN = 64
FLOPS = 2 * CONTRACTION * (2 * R * J + R * Q + N * O)


def tile_list_ctxboard_bank_store_plain_kernel(
    tc, xt_words, xt_scales, xo_words, xo_scales, w_words, w_scales, w0_words, w0_scales,
    xc_words, xc_scales, wg_words, wg_scales, vs_words, vs_scales,
    offs, offs2, offs3, offs4, offs5, offs6, offs7, out,
):
    nc = tc.nc
    with ExitStack() as ctx:
        sbuf = ctx.enter_context(tc.tile_pool(name="sbuf", bufs=1))
        psum = ctx.enter_context(tc.psum_pool(name="psum", bufs=1))

        def tile(name, shape, dtype):
            return sbuf.tile(shape, dtype, name=name, align_bytes=64)

        def quadrant(q, rows):
            return slice(QUAD * q, QUAD * q + rows)

        def columns(i):
            return slice(P * i, P * (i + 1))

        def zeroed_plane(name, width):
            plane = tile(name, [P, width], U8)
            nc.vector.memset(plane[:].bitcast(I32), 0)
            return plane

        def load_list(name, src):
            offsets = tile(name, list(src.shape), U16)
            nc.sync.dma_start(offsets[:], src)
            return offsets

        def load_fp8_words(name, src, queue):
            words = tile(name, [P, src.shape[2]], U32)
            queue.dma_start(words[:].bitcast(I32), src[0].rearrange("p n t -> p (n t)").bitcast(I32))
            return words

        def load_fp4_words(name, src, queue):
            words = tile(name, [P, src.shape[2] // 2], U16)
            queue.dma_start(words[:].bitcast(I32), src[0].bitcast(I32))
            return words

        def load_plane(plane, src):
            rows = src[0].bitcast(I32).rearrange("(q s) n -> s q n", s=LIVE)
            for s in range(LIVE):
                nc.sync.dma_start(plane[s:P:QUAD, :].bitcast(I32), rows[s])

        def load_staged(stage, first_column, src):
            rows = src[0].bitcast(I32).rearrange("(q s) n -> s q n", s=LIVE)
            nc.sync.dma_start(stage[:, :, first_column : first_column + src.shape[2]].bitcast(I32), rows)

        def move_rows(dst, src):
            nc.vector.tensor_copy(dst.bitcast(I32), src.bitcast(I32))

        def deal_words(name, words, dtype, word_bytes):
            dealt = tile(name, [P, R], dtype)
            run = LINE_BYTES // word_bytes
            nc.scalar.copy(
                dealt[:].rearrange("p (t c i) -> p c t i", t=PACK, i=run),
                words[:].rearrange("p (c i t) -> p c t i", t=PACK, i=run),
            )
            return dealt

        def deal_scales(name, engine, plane, first_slice, slices):
            dealt = tile(name, [P, slices, P], U8)
            by_slice = plane.rearrange("p (m t) -> p t m", t=PACK)
            engine.tensor_copy(dealt[:], by_slice[:, first_slice : first_slice + slices, :])
            return dealt

        def gather(name, table, offsets, entries, dtype):
            listed = tile(name, [P, entries], dtype)
            nc.vector.tensor_copy(listed[:], table[:].indirect(offsets[:]))
            return listed

        home = 2
        a_stage = tile("a_stage", [P, QUADS, 2 * R], U8)
        nc.vector.memset(a_stage[QUAD * home : P, 0 : home + 1, :].bitcast(I32), 0)
        g_plane = zeroed_plane("g_plane", R + Q)
        g_stage = tile("g_stage", [LIVE, QUADS, R + Q], U8)
        xt_plane = zeroed_plane("xt_plane", TABLE)
        xo_plane = zeroed_plane("xo_plane", TABLE)
        vs_plane = zeroed_plane("vs_plane", TABLE)
        boards = [tile("board%d" % t, [P, C], F32) for t in range(PACK)]
        for board in boards:
            nc.vector.memset(board[:], 0.0)

        load_staged(g_stage[:], 0, wg_scales)
        wg_loaded = load_fp8_words("wg_loaded", wg_words, nc.scalar)
        load_staged(g_stage[:], R, xc_scales)
        w0_loaded = load_fp4_words("w0_loaded", w0_words, nc.scalar)
        xc = load_fp8_words("xc", xc_words, nc.sync)
        w_loaded = load_fp8_words("w_loaded", w_words, nc.scalar)
        load_staged(a_stage[quadrant(home, LIVE)], 0, w_scales)
        load_staged(a_stage[quadrant(home, LIVE)], R, w0_scales)
        xt_table = load_fp4_words("xt_table", xt_words, nc.sync)
        token_list = load_list("token_list", offs)
        put_list = load_list("put_list", offs3)
        load_plane(xt_plane, xt_scales)
        xo_table = load_fp8_words("xo_table", xo_words, nc.sync)
        note_list = load_list("note_list", offs2)
        load_plane(xo_plane, xo_scales)
        take_list = load_list("take_list", offs4)
        vs_table = load_fp4_words("vs_table", vs_words, nc.sync)
        store_list = load_list("store_list", offs7)
        load_plane(vs_plane, vs_scales)
        first_list = load_list("first_list", offs5)
        second_list = load_list("second_list", offs6)

        for q in range(QUADS):
            move_rows(g_plane[quadrant(q, LIVE), :], g_stage[:, q, :])
        wg = deal_words("wg", wg_loaded, U32, 4)
        wg_scale = [
            deal_scales("wg_scale%d" % h, engine, g_plane[:, 0:R], PAIR * h, PAIR)
            for h, engine in enumerate((nc.vector, nc.gpsimd))
        ]
        g0 = tile("g0", [P, PACK, Q], F32)
        for h in range(PACK // PAIR):
            g_sums = psum.tile([P, PAIR, Q], F32, name="g_sums%d" % h)
            for u in range(PAIR):
                nc.tensor.matmul_mx(
                    out=g_sums[:, u, :],
                    lhsT=wg[:, columns(PAIR * h + u)].bitcast(E5M2), lhsT_scale=wg_scale[h][:, u, :],
                    rhs=xc[:].bitcast(E4M3), rhs_scale=g_plane[:, R : R + Q], start=True, stop=True,
                )
            nc.scalar.activation(g0[:, PAIR * h : PAIR * (h + 1), :], g_sums[:], COPY)

        xt_listed = gather("xt_listed", xt_table, token_list, J, U16)
        xt_scale = gather("xt_scale", xt_plane, token_list, J, U8)
        w = deal_words("w", w_loaded, U32, 4)
        for q in range(home):
            move_rows(a_stage[quadrant(q, QUAD), home, :], a_stage[quadrant(home, QUAD), q, :])
        move_rows(a_stage[quadrant(home + 1, LIVE), home, :], a_stage[quadrant(home, LIVE), home + 1, :])
        w_scale = deal_scales("w_scale", nc.gpsimd, a_stage[:, home, 0:R], 0, PACK)
        w0_scale = deal_scales("w0_scale", nc.gpsimd, a_stage[:, home, R : 2 * R], 0, PACK)
        w0 = deal_words("w0", w0_loaded, U16, 2)
        xo_listed = gather("xo_listed", xo_table, note_list, J, U32)
        xo_scale = gather("xo_scale", xo_plane, note_list, J, U8)

        vs_listed = gather("vs_listed", vs_table, store_list, N, U16)
        vs_scale = gather("vs_scale", vs_plane, store_list, N, U8)

        for t in range(PACK):
            nc.scalar.activation(boards[t][:].indirect(put_list[:]), g0[:, t, :], COPY)

        a = []
        for t in range(PACK):
            a_sums = psum.tile([P, J], F32, name="a_sums%d" % t)
            nc.tensor.matmul_mx(
                out=a_sums[:], lhsT=w[:, columns(t)].bitcast(E4M3), lhsT_scale=w_scale[:, t, :],
                rhs=xt_listed[:].bitcast(E2M1), rhs_scale=xt_scale[:], start=True, stop=False,
            )
            nc.tensor.matmul_mx(
                out=a_sums[:], lhsT=w0[:, columns(t)].bitcast(E2M1), lhsT_scale=w0_scale[:, t, :],
                rhs=xo_listed[:].bitcast(E4M3), rhs_scale=xo_scale[:], start=False, stop=True,
            )
            a_slice = tile("a%d" % t, [P, J], F32)
            nc.vector.tensor_copy(a_slice[:], a_sums[:])
            a.append(a_slice)

        taken = tile("taken", [P, PACK, O], F32)
        first = tile("first", [P, PACK, O], F32)
        second = tile("second", [P, PACK, O], F32)
        larger = tile("larger", [P, PACK, O], F32)
        hid = tile("hid", [P, O, PACK], BF16)
        for t in range(PACK):
            nc.vector.tensor_copy(taken[:, t, :], boards[t][:].indirect(take_list[:]))
        for h in range(PACK // PAIR):
            pair = slice(PAIR * h, PAIR * (h + 1))
            for t in range(pair.start, pair.stop):
                nc.scalar.activation(first[:, t, :], a[t][:].indirect(first_list[:]), COPY, scale=g0[:, t, 0:1])
                nc.scalar.activation(
                    second[:, t, :], a[t][:].indirect(second_list[:]), COPY, scale=g0[:, t, GB_COLUMN : GB_COLUMN + 1]
                )
                nc.vector.tensor_tensor(larger[:, t, :], first[:, t, :], second[:, t, :], ALU.max)
            nc.vector.tensor_tensor(
                hid[:, :, pair],
                larger[:, pair, :].rearrange("p t o -> p o t"),
                taken[:, pair, :].rearrange("p t o -> p o t"),
                ALU.subtract,
            )

        hid_words = tile("hid_words", [P, O], U32)
        hid_scale = tile("hid_scale", [P, O], U8)
        nc.vector.quantize_mx(
            out=hid_words[:].bitcast(E5M2), scales=hid_scale[:], in_=hid[:].rearrange("p o t -> p (o t)")
        )

        y = tile("y", [P, N // P, O], F32)
        for half, (copy, queue) in enumerate(((nc.vector.tensor_copy, nc.sync), (nc.scalar.copy, nc.scalar))):
            y_sums = psum.tile([P, O], F32, name="y_sums%d" % half)
            nc.tensor.matmul_mx(
                out=y_sums[:], lhsT=vs_listed[:, columns(half)].bitcast(E2M1), lhsT_scale=vs_scale[:, columns(half)],
                rhs=hid_words[:].bitcast(E5M2), rhs_scale=hid_scale[:], start=True, stop=True,
            )
            copy(y[:, half, :], y_sums[:])
            queue.dma_start(out[columns(half), :], y[:, half, :])
